import numpy as np
import ml_dtypes

BF16 = ml_dtypes.bfloat16


def bf(x):
    return np.asarray(x, np.float32).astype(BF16)


def f32(x):
    return np.asarray(x, np.float32)


def f64(x):
    return np.asarray(x).astype(np.float64)


def striped(idx):
    return np.tile(idx.reshape(-1, 16).T, (8, 1))


S, K, M, N, E, Q = 512, 128, 256, 512, 4, 128


def setup_inputs():
    return {"base": bf(np.random.standard_normal((M, S))), "x": bf(np.random.standard_normal((K, N))), "w": bf(np.random.standard_normal((E, K, M)) / np.sqrt(K)), "offs": striped(np.random.permutation(S))}


def reference(base, x, w, offs):
    idx = offs[:16].T.reshape(-1)
    z = f64(base).copy()
    for e in range(E):
        z[:, idx[e * Q : (e + 1) * Q]] += f64(w)[e].T @ f64(x)[:, e * Q : (e + 1) * Q]
    return z

@@ -1,0 +1,57 @@
+import concourse.mybir as mybir
+from concourse.masks import make_identity
+
+BF16, F32, U16 = mybir.dt.bfloat16, mybir.dt.float32, mybir.dt.uint16
+
+P = 128
+TOKENS = 512
+EXPERTS = 4
+PIECE = TOKENS // EXPERTS
+FEATURES = 256
+BLOCKS = FEATURES // P
+PIECE_COLS = PIECE // 16
+
+FLOPS = 2 * P * FEATURES * TOKENS
+
+
+def tile_scatter_matmul_kernel(tc, base, x, w, offs, out):
+    nc = tc.nc
+    with (
+        tc.tile_pool(name="held", bufs=1) as held,
+        tc.psum_pool(name="banks", bufs=1) as banks,
+    ):
+        offsets = held.tile([P, TOKENS // 16], U16, name="offsets")
+        nc.sync.dma_start(offsets[:], offs)
+
+        base_tiles = [held.tile([P, TOKENS], BF16, name=f"base{b}") for b in range(BLOCKS)]
+        for b in range(BLOCKS):
+            nc.scalar.dma_start(base_tiles[b][:], base[b * P : (b + 1) * P, :])
+
+        x_tile = held.tile([P, TOKENS], BF16, name="x_tile")
+        nc.sync.dma_start(x_tile[:], x)
+
+        w_tile = held.tile([P, EXPERTS, FEATURES], BF16, name="w_tile")
+        nc.gpsimd.dma_start(w_tile[:], w.rearrange("e k m -> k e m"))
+
+        identity = held.tile([P, P], BF16, name="identity")
+        make_identity(nc, identity[:])
+
+        windows = [banks.tile([P, TOKENS], F32, name=f"window{b}") for b in range(BLOCKS)]
+        for b in range(BLOCKS):
+            nc.tensor.matmul(windows[b][:], identity[:], base_tiles[b][:], start=True, stop=False)
+
+        for b in range(BLOCKS):
+            for e in range(EXPERTS):
+                nc.tensor.matmul(
+                    windows[b][:].indirect(offsets[:, e * PIECE_COLS : (e + 1) * PIECE_COLS]),
+                    w_tile[:, e, b * P : (b + 1) * P],
+                    x_tile[:, e * PIECE : (e + 1) * PIECE],
+                    start=False,
+                    stop=(e == EXPERTS - 1),
+                )
+
+        for b in range(BLOCKS):
+            z_tile = held.tile([P, TOKENS], F32, name=f"z{b}")
+            nc.vector.tensor_copy(z_tile[:], windows[b][:])
+            store_queue = nc.sync if b % 2 == 0 else nc.scalar
+            store_queue.dma_start(out[b * P : (b + 1) * P, :], z_tile[:])

@@ -20,18 +20,19 @@ def tile_scatter_matmul_kernel(tc, base, x, w, offs, out):
         tc.tile_pool(name="held", bufs=1) as held,
         tc.psum_pool(name="banks", bufs=1) as banks,
     ):
-        offsets = held.tile([P, TOKENS // 16], U16, name="offsets")
-        nc.sync.dma_start(offsets[:], offs)
-
+        queues = [nc.sync, nc.scalar]
         base_tiles = [held.tile([P, TOKENS], BF16, name=f"base{b}") for b in range(BLOCKS)]
         for b in range(BLOCKS):
-            nc.scalar.dma_start(base_tiles[b][:], base[b * P : (b + 1) * P, :])
+            queues[b].dma_start(base_tiles[b][:], base[b * P : (b + 1) * P, :])
+
+        offsets = held.tile([P, TOKENS // 16], U16, name="offsets")
+        nc.sync.dma_start(offsets[:], offs)
 
         x_tile = held.tile([P, TOKENS], BF16, name="x_tile")
         nc.sync.dma_start(x_tile[:], x)
 
         w_tile = held.tile([P, EXPERTS, FEATURES], BF16, name="w_tile")
-        nc.gpsimd.dma_start(w_tile[:], w.rearrange("e k m -> k e m"))
+        nc.scalar.dma_start(w_tile[:], w.rearrange("e k m -> k e m"))
 
         identity = held.tile([P, P], BF16, name="identity")
         make_identity(nc, identity[:])
@@ -52,6 +53,8 @@ def tile_scatter_matmul_kernel(tc, base, x, w, offs, out):
 
         for b in range(BLOCKS):
             z_tile = held.tile([P, TOKENS], F32, name=f"z{b}")
-            nc.vector.tensor_copy(z_tile[:], windows[b][:])
-            store_queue = nc.sync if b % 2 == 0 else nc.scalar
-            store_queue.dma_start(out[b * P : (b + 1) * P, :], z_tile[:])
+            if b == 0:
+                nc.vector.tensor_copy(z_tile[:], windows[b][:])
+            else:
+                nc.scalar.copy(z_tile[:], windows[b][:])
+            queues[b].dma_start(out[b * P : (b + 1) * P, :], z_tile[:])

@@ -10,6 +10,7 @@ PIECE = TOKENS // EXPERTS
 FEATURES = 256
 BLOCKS = FEATURES // P
 PIECE_COLS = PIECE // 16
+WARM_MATMULS = 4
 
 FLOPS = 2 * P * FEATURES * TOKENS
 
@@ -33,6 +34,12 @@ def tile_scatter_matmul_kernel(tc, base, x, w, offs, out):
 
         w_tile = held.tile([P, EXPERTS, FEATURES], BF16, name="w_tile")
         nc.scalar.dma_start(w_tile[:], w.rearrange("e k m -> k e m"))
+
+        zeros = held.tile([P, TOKENS], BF16, name="zeros")
+        nc.vector.memset(zeros[:], 0.0)
+        unread = banks.tile([P, TOKENS], F32, name="unread")
+        for i in range(WARM_MATMULS):
+            nc.tensor.matmul(unread[:], zeros[:, :P], zeros[:], start=True, stop=True)
 
         identity = held.tile([P, P], BF16, name="identity")
         make_identity(nc, identity[:])

@@ -10,6 +10,7 @@ PIECE = TOKENS // EXPERTS
 FEATURES = 256
 BLOCKS = FEATURES // P
 PIECE_COLS = PIECE // 16
+PAIR = 2
 WARM_MATMULS = 4
 
 FLOPS = 2 * P * FEATURES * TOKENS
@@ -30,10 +31,11 @@ def tile_scatter_matmul_kernel(tc, base, x, w, offs, out):
         nc.sync.dma_start(offsets[:], offs)
 
         x_tile = held.tile([P, TOKENS], BF16, name="x_tile")
-        nc.sync.dma_start(x_tile[:], x)
+        nc.scalar.dma_start(x_tile[:], x)
 
-        w_tile = held.tile([P, EXPERTS, FEATURES], BF16, name="w_tile")
-        nc.scalar.dma_start(w_tile[:], w.rearrange("e k m -> k e m"))
+        w_tiles = [held.tile([P, PAIR, FEATURES], BF16, name=f"w_pair{h}") for h in range(EXPERTS // PAIR)]
+        for h in range(EXPERTS // PAIR):
+            queues[h].dma_start(w_tiles[h][:], w[h * PAIR : (h + 1) * PAIR].rearrange("e k m -> k e m"))
 
         zeros = held.tile([P, TOKENS], BF16, name="zeros")
         nc.vector.memset(zeros[:], 0.0)
@@ -52,7 +54,7 @@ def tile_scatter_matmul_kernel(tc, base, x, w, offs, out):
             for e in range(EXPERTS):
                 nc.tensor.matmul(
                     windows[b][:].indirect(offsets[:, e * PIECE_COLS : (e + 1) * PIECE_COLS]),
-                    w_tile[:, e, b * P : (b + 1) * P],
+                    w_tiles[e // PAIR][:, e % PAIR, b * P : (b + 1) * P],
                     x_tile[:, e * PIECE : (e + 1) * PIECE],
                     start=False,
                     stop=(e == EXPERTS - 1),

@@ -11,6 +11,7 @@ FEATURES = 256
 BLOCKS = FEATURES // P
 PIECE_COLS = PIECE // 16
 PAIR = 2
+ROW_ALIGN = 256
 WARM_MATMULS = 4
 
 FLOPS = 2 * P * FEATURES * TOKENS
@@ -23,17 +24,20 @@ def tile_scatter_matmul_kernel(tc, base, x, w, offs, out):
         tc.psum_pool(name="banks", bufs=1) as banks,
     ):
         queues = [nc.sync, nc.scalar]
-        base_tiles = [held.tile([P, TOKENS], BF16, name=f"base{b}") for b in range(BLOCKS)]
+        base_tiles = [held.tile([P, TOKENS], BF16, name=f"base{b}", align_bytes=ROW_ALIGN) for b in range(BLOCKS)]
         for b in range(BLOCKS):
             queues[b].dma_start(base_tiles[b][:], base[b * P : (b + 1) * P, :])
 
         offsets = held.tile([P, TOKENS // 16], U16, name="offsets")
         nc.sync.dma_start(offsets[:], offs)
 
-        x_tile = held.tile([P, TOKENS], BF16, name="x_tile")
+        x_tile = held.tile([P, TOKENS], BF16, name="x_tile", align_bytes=ROW_ALIGN)
         nc.scalar.dma_start(x_tile[:], x)
 
-        w_tiles = [held.tile([P, PAIR, FEATURES], BF16, name=f"w_pair{h}") for h in range(EXPERTS // PAIR)]
+        w_tiles = [
+            held.tile([P, PAIR, FEATURES], BF16, name=f"w_pair{h}", align_bytes=ROW_ALIGN)
+            for h in range(EXPERTS // PAIR)
+        ]
         for h in range(EXPERTS // PAIR):
             queues[h].dma_start(w_tiles[h][:], w[h * PAIR : (h + 1) * PAIR].rearrange("e k m -> k e m"))
 
@@ -61,7 +65,7 @@ def tile_scatter_matmul_kernel(tc, base, x, w, offs, out):
                 )
 
         for b in range(BLOCKS):
-            z_tile = held.tile([P, TOKENS], F32, name=f"z{b}")
+            z_tile = held.tile([P, TOKENS], F32, name=f"z{b}", align_bytes=ROW_ALIGN)
             if b == 0:
                 nc.vector.tensor_copy(z_tile[:], windows[b][:])
             else:

@@ -41,11 +41,17 @@ def tile_scatter_matmul_kernel(tc, base, x, w, offs, out):
         for h in range(EXPERTS // PAIR):
             queues[h].dma_start(w_tiles[h][:], w[h * PAIR : (h + 1) * PAIR].rearrange("e k m -> k e m"))
 
-        zeros = held.tile([P, TOKENS], BF16, name="zeros")
+        zeros = held.tile([P, 2], BF16, name="zeros")
         nc.vector.memset(zeros[:], 0.0)
         unread = banks.tile([P, TOKENS], F32, name="unread")
         for i in range(WARM_MATMULS):
-            nc.tensor.matmul(unread[:], zeros[:, :P], zeros[:], start=True, stop=True)
+            nc.tensor.matmul(
+                unread[:],
+                zeros[:, 0:1].to_broadcast([P, P]),
+                zeros[:, 0:1].to_broadcast([P, TOKENS]),
+                start=True,
+                stop=True,
+            )
 
         identity = held.tile([P, P], BF16, name="identity")
         make_identity(nc, identity[:])

@@ -12,7 +12,7 @@ BLOCKS = FEATURES // P
 PIECE_COLS = PIECE // 16
 PAIR = 2
 ROW_ALIGN = 256
-WARM_MATMULS = 4
+WARM_MATMULS = 3
 
 FLOPS = 2 * P * FEATURES * TOKENS
 

@@ -32,14 +32,14 @@ def tile_scatter_matmul_kernel(tc, base, x, w, offs, out):
         nc.sync.dma_start(offsets[:], offs)
 
         x_tile = held.tile([P, TOKENS], BF16, name="x_tile", align_bytes=ROW_ALIGN)
-        nc.scalar.dma_start(x_tile[:], x)
+        nc.sync.dma_start(x_tile[:], x)
 
         w_tiles = [
             held.tile([P, PAIR, FEATURES], BF16, name=f"w_pair{h}", align_bytes=ROW_ALIGN)
             for h in range(EXPERTS // PAIR)
         ]
         for h in range(EXPERTS // PAIR):
-            queues[h].dma_start(w_tiles[h][:], w[h * PAIR : (h + 1) * PAIR].rearrange("e k m -> k e m"))
+            nc.scalar.dma_start(w_tiles[h][:], w[h * PAIR : (h + 1) * PAIR].rearrange("e k m -> k e m"))
 
         zeros = held.tile([P, 2], BF16, name="zeros")
         nc.vector.memset(zeros[:], 0.0)

@@ -12,7 +12,7 @@ BLOCKS = FEATURES // P
 PIECE_COLS = PIECE // 16
 PAIR = 2
 ROW_ALIGN = 256
-WARM_MATMULS = 3
+WARM_MATMULS = 2
 
 FLOPS = 2 * P * FEATURES * TOKENS
 

import concourse.mybir as mybir
from concourse.masks import make_identity

BF16, F32, U16 = mybir.dt.bfloat16, mybir.dt.float32, mybir.dt.uint16

P = 128
TOKENS = 512
EXPERTS = 4
PIECE = TOKENS // EXPERTS
FEATURES = 256
BLOCKS = FEATURES // P
PIECE_COLS = PIECE // 16
PAIR = 2
ROW_ALIGN = 256
WARM_MATMULS = 2

FLOPS = 2 * P * FEATURES * TOKENS


def tile_scatter_matmul_kernel(tc, base, x, w, offs, out):
    nc = tc.nc
    with (
        tc.tile_pool(name="held", bufs=1) as held,
        tc.psum_pool(name="banks", bufs=1) as banks,
    ):
        queues = [nc.sync, nc.scalar]
        base_tiles = [held.tile([P, TOKENS], BF16, name=f"base{b}", align_bytes=ROW_ALIGN) for b in range(BLOCKS)]
        for b in range(BLOCKS):
            queues[b].dma_start(base_tiles[b][:], base[b * P : (b + 1) * P, :])

        offsets = held.tile([P, TOKENS // 16], U16, name="offsets")
        nc.sync.dma_start(offsets[:], offs)

        x_tile = held.tile([P, TOKENS], BF16, name="x_tile", align_bytes=ROW_ALIGN)
        nc.sync.dma_start(x_tile[:], x)

        w_tiles = [
            held.tile([P, PAIR, FEATURES], BF16, name=f"w_pair{h}", align_bytes=ROW_ALIGN)
            for h in range(EXPERTS // PAIR)
        ]
        for h in range(EXPERTS // PAIR):
            nc.scalar.dma_start(w_tiles[h][:], w[h * PAIR : (h + 1) * PAIR].rearrange("e k m -> k e m"))

        zeros = held.tile([P, 2], BF16, name="zeros")
        nc.vector.memset(zeros[:], 0.0)
        unread = banks.tile([P, TOKENS], F32, name="unread")
        for i in range(WARM_MATMULS):
            nc.tensor.matmul(
                unread[:],
                zeros[:, 0:1].to_broadcast([P, P]),
                zeros[:, 0:1].to_broadcast([P, TOKENS]),
                start=True,
                stop=True,
            )

        identity = held.tile([P, P], BF16, name="identity")
        make_identity(nc, identity[:])

        windows = [banks.tile([P, TOKENS], F32, name=f"window{b}") for b in range(BLOCKS)]
        for b in range(BLOCKS):
            nc.tensor.matmul(windows[b][:], identity[:], base_tiles[b][:], start=True, stop=False)

        for b in range(BLOCKS):
            for e in range(EXPERTS):
                nc.tensor.matmul(
                    windows[b][:].indirect(offsets[:, e * PIECE_COLS : (e + 1) * PIECE_COLS]),
                    w_tiles[e // PAIR][:, e % PAIR, b * P : (b + 1) * P],
                    x_tile[:, e * PIECE : (e + 1) * PIECE],
                    start=False,
                    stop=(e == EXPERTS - 1),
                )

        for b in range(BLOCKS):
            z_tile = held.tile([P, TOKENS], F32, name=f"z{b}", align_bytes=ROW_ALIGN)
            if b == 0:
                nc.vector.tensor_copy(z_tile[:], windows[b][:])
            else:
                nc.scalar.copy(z_tile[:], windows[b][:])
            queues[b].dma_start(out[b * P : (b + 1) * P, :], z_tile[:])
